import numpy as np
import ml_dtypes


def mxq(x, axis, fmt="e4m3"):
    dtype, down = {"e4m3": (ml_dtypes.float8_e4m3fn, 7), "e5m2": (ml_dtypes.float8_e5m2, 14)}[fmt]
    v = np.moveaxis(np.asarray(x, np.float32).astype(ml_dtypes.bfloat16).astype(np.float64), axis, -1)
    blocks = v.reshape(v.shape[:-1] + (-1, 32))
    amax = np.abs(blocks).max(-1, keepdims=True)
    byte = np.maximum(np.where(amax > 0, np.frexp(amax)[1] - 1 + 127, 0) - down, 1)
    scale = np.exp2(byte - 127.0)
    codes = (blocks / scale).astype(np.float32).astype(dtype).astype(np.float64)
    return np.moveaxis((codes * scale).reshape(v.shape), -1, axis)


WIDE = False


def mx_kscale(k):
    if not WIDE:
        return np.ones(k)
    levels = np.array([10, -10, 5, -5, 0])
    if k % 512:
        return np.exp2(np.random.permutation(np.resize(levels, k // 32))).repeat(32)
    a = np.empty((k // 512, 16))
    for p in range(k // 512):
        a[p, :8] = np.random.permutation(np.resize(levels, 8))
        for g in range(8):
            far = levels[np.abs(levels - a[p, g]) >= 10]
            a[p, g + 8] = far[np.random.randint(len(far))]
    return np.exp2(a.ravel()).repeat(32)


def f64(x):
    return np.asarray(x).astype(np.float64)


def striped(idx):
    return np.tile(idx.reshape(-1, 16).T, (8, 1)).astype(np.uint16)


def unstriped(offs):
    return offs[:16].T.reshape(-1).astype(np.int64)


def pack_weight(w):
    k, n = w.shape
    w = f64(np.asarray(w, np.float32).astype(ml_dtypes.bfloat16)).reshape(k // 32, 32, n)
    amax = np.abs(w).max(1)
    byte = np.clip(np.where(amax > 0, np.frexp(amax)[1] - 1 + 127 - 7, 1), 1, 254)
    scaled = (w * np.exp2(127.0 - byte)[:, None, :]).reshape(k, n).astype(np.float32)
    words = np.ascontiguousarray(scaled.reshape(k // 512, 128, 4, n).transpose(0, 1, 3, 2)).astype(ml_dtypes.float8_e4m3fn).view(np.uint8)
    return words, np.ascontiguousarray(byte.astype(np.uint8).reshape(k // 512, 16, n))


def unpack_weight(words, scales):
    g, p, n, _ = words.shape
    vals = np.ascontiguousarray(words).view(ml_dtypes.float8_e4m3fn).astype(np.float64) * np.repeat(np.exp2(scales.astype(np.float64) - 127.0), 8, axis=1)[..., None]
    return vals.transpose(0, 1, 3, 2).reshape(g * 512, n)


def gelu(v):
    return 0.5 * v * (1.0 + np.tanh(np.sqrt(2.0 / np.pi) * (v + 0.044715 * v**3)))


K, T, S, N, H, W, G, U = 512, 2048, 512, 256, 512, 2048, 1024, 1024


def setup_inputs():
    n = np.random.standard_normal
    s = mx_kscale(K)[:, None]
    u = mx_kscale(H)
    packed_xT = pack_weight(n((K, T)) * s)
    packed_eT = pack_weight(n((K, W)) * s)
    packed_dT = pack_weight(n((K, G)) * s)
    return {
        "x_words": packed_xT[0],
        "x_scales": packed_xT[1],
        "w1": (n((K, H)) / np.sqrt(K) / s).astype(np.float32),
        "e_words": packed_eT[0],
        "e_scales": packed_eT[1],
        "w2": (n((K, H)) / np.sqrt(K) / s).astype(np.float32),
        "d_words": packed_dT[0],
        "d_scales": packed_dT[1],
        "w3": (n((K, H)) / np.sqrt(K) / s).astype(np.float32),
        "unit": (np.random.uniform(0.6, 1.4, (H, 1)) * u[:, None]).astype(np.float32),
        "w4": (n((H, N)) / np.sqrt(H) / u[:, None]).astype(np.float32),
        "offs": striped(np.random.permutation(T)[:S]),
        "gra": striped(np.random.permutation(W)[:S]),
        "grb": striped(np.random.permutation(G)[:S]),
        "sc_": striped(np.random.permutation(np.concatenate([np.arange(S), np.random.randint(0, S, U - S)]))),
        "ra": striped(np.random.permutation(np.concatenate([np.arange(S), np.random.randint(0, S, U - S)]))),
        "rb": striped(np.random.permutation(np.concatenate([np.arange(S), np.random.randint(0, S, U - S)]))),
    }


def reference(x_words, x_scales, w1, e_words, e_scales, w2, d_words, d_scales, w3, unit, w4, offs, gra, grb, sc_, ra, rb):
    xq = unpack_weight(x_words, x_scales)[:, unstriped(offs)]
    y = mxq(f64(w1), 0, "e4m3").T @ xq
    ys1 = y[:, unstriped(sc_)]
    e_gra = unpack_weight(e_words, e_scales)[:, unstriped(gra)]
    ye = mxq(f64(w2), 0, "e4m3").T @ e_gra
    ea = ye[:, unstriped(ra)]
    d_grb = unpack_weight(d_words, d_scales)[:, unstriped(grb)]
    yd = mxq(f64(w3), 0, "e4m3").T @ d_grb
    db = yd[:, unstriped(rb)]
    clash = np.minimum(ea, db)
    mol = ys1 + ea + db - (1.3 * clash)
    hid = f64(unit) * gelu(mol)
    return mxq(f64(w4), 0, "e4m3").T @ mxq(hid, 0, "e4m3")

@@ -1,0 +1,255 @@
+from contextlib import ExitStack
+
+import concourse.mybir as mybir
+from concourse.masks import make_identity
+
+K, S, N, H, U = 512, 512, 256, 512, 1024
+FLOPS = 2 * (3 * K * H * S + H * N * U)
+
+F32 = mybir.dt.float32
+BF16 = mybir.dt.bfloat16
+I32 = mybir.dt.int32
+U32 = mybir.dt.uint32
+U16 = mybir.dt.uint16
+U8 = mybir.dt.uint8
+FP8X4 = mybir.dt.float8_e4m3fn_x4
+ALU = mybir.AluOpType
+ACT = mybir.ActivationFunctionType
+
+P = 128
+PACK = 4
+STRIPE = 16
+CHUNK_BLOCKS = (2, 2, 2, 2)
+GROUP_BLOCKS = (2, 2, 2, 1, 1)
+
+
+def tile_picked_yscafld_gelu_p_kernel(
+    tc, x_words, x_scales, w1, e_words, e_scales, w2, d_words, d_scales, w3, unit, w4, offs, gra, grb, sc_, ra, rb, out
+):
+    nc = tc.nc
+    with ExitStack() as ctx:
+        keep = ctx.enter_context(tc.tile_pool(name="keep", bufs=1))
+        ring = ctx.enter_context(tc.tile_pool(name="ring", bufs=3))
+        prod_psum = ctx.enter_context(tc.psum_pool(name="prod_psum", bufs=2))
+        sum_psum = ctx.enter_context(tc.psum_pool(name="sum_psum", bufs=4))
+        back_psum = ctx.enter_context(tc.psum_pool(name="back_psum", bufs=2))
+
+        def load_list(name, src):
+            tile = keep.tile(list(src.shape), U16, name=name)
+            nc.sync.dma_start(tile[:], src)
+            return tile
+
+        def load_words(name, src):
+            tile = keep.tile([P, src.shape[2]], I32, name=name + "_words", align_bytes=64)
+            nc.sync.dma_start(tile[:], src[0].rearrange("p c r -> p (c r)").bitcast(I32))
+            return tile
+
+        def clear_scales(name, src):
+            tile = keep.tile([P, src.shape[2]], U8, name=name + "_scales", align_bytes=64)
+            nc.vector.memset(tile[:].bitcast(I32), 0)
+            return tile
+
+        def load_scales(tile, src):
+            for row in range(4):
+                nc.sync.dma_start(tile[row:P:32, :].bitcast(I32), src[0, row:16:4, :].bitcast(I32))
+
+        def load_scales_everywhere(name, src):
+            tile = keep.tile([P, src.shape[2]], U8, name=name + "_scales", align_bytes=64)
+            for quad in range(4):
+                rows = src[0, 4 * quad : 4 * quad + 4, :].bitcast(I32)
+                nc.sync.dma_start(
+                    tile[32 * quad : 32 * quad + 32, :].bitcast(I32), rows.unsqueeze(0).to_broadcast([8] + list(rows.shape))
+                )
+            return tile
+
+        def load_weight(name, src):
+            tile = keep.tile([P, PACK, src.shape[1]], F32, name=name + "_raw", align_bytes=64)
+            nc.sync.dma_start(tile[:], src.rearrange("(p j) c -> p j c", j=PACK))
+            return tile
+
+        def pick_columns(name, words, scales, offsets):
+            codes = keep.tile([P, S], U32, name=name + "_codes", align_bytes=64)
+            nc.vector.tensor_copy(codes[:], words[:].bitcast(U32).indirect(offsets[:]))
+            plane = keep.tile([P, S], U8, name=name + "_plane", align_bytes=64)
+            nc.vector.tensor_copy(plane[:], scales[:].indirect(offsets[:]))
+            return codes, plane
+
+        def quantize(name, rounded):
+            width = rounded.shape[1] // PACK
+            codes = keep.tile([P, width], U32, name=name + "_codes", tag=name + "_codes", align_bytes=64)
+            plane = keep.tile([P, width], U8, name=name + "_plane", align_bytes=64)
+            nc.vector.quantize_mx(out=codes[:].bitcast(FP8X4), scales=plane[:], in_=rounded)
+            return codes, plane
+
+        def dealt_views(name, raw):
+            rounded = keep.tile([P, H * PACK], BF16, name=name + "_bf16", align_bytes=64)
+            dst = rounded[:].rearrange("p (t m j) -> p m j t", t=PACK, j=PACK)
+            src = raw[:].rearrange("p j (m t) -> p m j t", t=PACK)
+            return rounded, dst, src
+
+        def product_tile(name, t, weight, picked, engine, pool):
+            cols = slice(t * P, (t + 1) * P)
+            bank = pool.tile([P, S], F32, name="bank")
+            nc.tensor.matmul_mx(
+                out=bank[:],
+                lhsT=weight[0][:, cols].bitcast(FP8X4),
+                lhsT_scale=weight[1][:, cols],
+                rhs=picked[0][:].bitcast(FP8X4),
+                rhs_scale=picked[1][:],
+                start=True,
+                stop=True,
+            )
+            window = keep.tile([P, S], F32, name="%s_%d" % (name, t), align_bytes=64)
+            if engine is nc.scalar:
+                nc.scalar.copy(window[:], bank[:])
+            else:
+                nc.vector.tensor_copy(window[:], bank[:])
+            return window
+
+        starts = [P * sum(CHUNK_BLOCKS[:c]) for c in range(len(CHUNK_BLOCKS))]
+        widths = [P * blocks for blocks in CHUNK_BLOCKS]
+
+        def chunk_offsets(offsets, c):
+            return offsets[:, starts[c] // STRIPE : (starts[c] + widths[c]) // STRIPE]
+
+        def chunk_tile(c):
+            return ring.tile([P, 3, PACK, widths[c]], F32, name="work", bufs=2, align_bytes=64)
+
+        def fetch(dst, t, window, offsets, c):
+            nc.scalar.activation(dst[:, t, :], window[:].indirect(chunk_offsets(offsets, c)), ACT.Copy)
+
+        e_scale_tile = clear_scales("e", e_scales)
+        x_scale_tile = clear_scales("x", x_scales)
+
+        d_word_tile = load_words("d", d_words)
+        grb_list = load_list("grb_list", grb)
+        d_scale_tile = load_scales_everywhere("d", d_scales)
+        w3_raw = load_weight("w3", w3)
+        e_word_tile = load_words("e", e_words)
+        gra_list = load_list("gra_list", gra)
+        rb_list = load_list("rb_list", rb)
+        load_scales(e_scale_tile, e_scales)
+        w2_raw = load_weight("w2", w2)
+        x_word_tile = load_words("x", x_words)
+        offs_list = load_list("offs_list", offs)
+        ra_list = load_list("ra_list", ra)
+        load_scales(x_scale_tile, x_scales)
+        w1_raw = load_weight("w1", w1)
+        sc_list = load_list("sc_list", sc_)
+        w4_raw = load_weight("w4", w4)
+        unit_tile = keep.tile([P, PACK], F32, name="unit_tile")
+        nc.sync.dma_start(unit_tile[:], unit.rearrange("(p t) o -> p (t o)", t=PACK))
+
+        identity = keep.tile([P, P], F32, name="identity")
+        make_identity(nc, identity[:])
+
+        chunks = range(len(CHUNK_BLOCKS))
+        work = [chunk_tile(0)]
+        ea = [work[0][:, 0]]
+        db = [work[0][:, 1]]
+
+        d_picked = pick_columns("d_picked", d_word_tile, d_scale_tile, grb_list)
+        rounded, dst, src = dealt_views("w3", w3_raw)
+        nc.scalar.copy(dst[:, :48], src[:, :48])
+        nc.vector.tensor_copy(dst[:, 48:], src[:, 48:])
+        w3_q = quantize("w3", rounded[:])
+        yd = [product_tile("yd", t, w3_q, d_picked, engine, (sum_psum, sum_psum, sum_psum, sum_psum)[t]) for t, engine in enumerate((nc.scalar, nc.scalar, nc.scalar, nc.scalar))]
+        for t in range(PACK):
+            fetch(db[0], t, yd[t], rb_list, 0)
+
+        e_picked = pick_columns("e_picked", e_word_tile, e_scale_tile, gra_list)
+        rounded, dst, src = dealt_views("w2", w2_raw)
+        nc.vector.tensor_copy(dst, src)
+        w2_q = quantize("w2", rounded[:])
+        ye = [product_tile("ye", t, w2_q, e_picked, engine, (prod_psum, prod_psum, back_psum, back_psum)[t]) for t, engine in enumerate((nc.scalar, nc.scalar, nc.scalar, nc.scalar))]
+        for t in range(PACK):
+            fetch(ea[0], t, ye[t], ra_list, 0)
+
+        x_picked = pick_columns("x_picked", x_word_tile, x_scale_tile, offs_list)
+        rounded, dst, src = dealt_views("w1", w1_raw)
+        nc.vector.tensor_copy(dst, src)
+        w1_q = quantize("w1", rounded[:])
+        y = [product_tile("y", t, w1_q, x_picked, engine, (sum_psum, sum_psum, sum_psum, sum_psum)[t]) for t, engine in enumerate((nc.vector, nc.vector, nc.vector, nc.vector))]
+
+        rounded = keep.tile([P, N * PACK], BF16, name="w4_bf16", align_bytes=64)
+        dst = rounded[:].rearrange("p (c i j) -> p c j i", i=4, j=PACK)
+        src = w4_raw[:].rearrange("p j (c i) -> p c j i", i=4)
+        nc.vector.tensor_copy(dst, src)
+        w4_q = quantize("w4", rounded[:])
+
+        group_of = [g for g, blocks in enumerate(GROUP_BLOCKS) for b in range(blocks)]
+        group_start = [sum(GROUP_BLOCKS[:g]) for g in range(len(GROUP_BLOCKS))]
+        hid = [
+            keep.tile([P, blocks * P * PACK], BF16, name="hid%d" % g, align_bytes=64) for g, blocks in enumerate(GROUP_BLOCKS)
+        ]
+        unit_spread = unit_tile[:].unsqueeze(1).to_broadcast([P, P, PACK])
+        out_view = out.rearrange("(h p) r -> p h r", p=P)
+
+        def finish_block(block, parts):
+            total = sum_psum.tile([P, PACK, P], F32, name="total", tag="bank")
+            for k, part in enumerate(parts):
+                for t in range(PACK):
+                    nc.tensor.matmul(
+                        total[:, t, :],
+                        part[:, t, :],
+                        identity[:],
+                        start=(k == 0 and t == 0),
+                        stop=(k == len(parts) - 1 and t == PACK - 1),
+                        is_transpose=True,
+                    )
+            smooth = ring.tile([P, PACK, P], F32, name="smooth", align_bytes=64)
+            nc.scalar.activation(smooth[:], total[:], ACT.Gelu_apprx_tanh)
+            back = back_psum.tile([P, PACK, P], F32, name="back", tag="bank")
+            for t in range(PACK):
+                nc.tensor.transpose(back[:, t, :], smooth[:, t, :], identity[:])
+            g = group_of[block]
+            place = block - group_start[g]
+            dst = hid[g][:, place * P * PACK : (place + 1) * P * PACK].rearrange("p (r t) -> p r t", t=PACK)
+            nc.vector.tensor_tensor(dst, back[:].rearrange("p t r -> p r t"), unit_spread, ALU.mult)
+
+        def finish_group(g):
+            width = GROUP_BLOCKS[g] * P
+            codes, plane = quantize("hid%d" % g, hid[g][:])
+            bank = prod_psum.tile([P, N // P, width], F32, name="result", tag="bank")
+            for h in range(N // P):
+                cols = slice(h * P, (h + 1) * P)
+                nc.tensor.matmul_mx(
+                    out=bank[:, h, :],
+                    lhsT=w4_q[0][:, cols].bitcast(FP8X4),
+                    lhsT_scale=w4_q[1][:, cols],
+                    rhs=codes[:].bitcast(FP8X4),
+                    rhs_scale=plane[:],
+                    start=True,
+                    stop=True,
+                )
+            staged = ring.tile([P, N // P, width], F32, name="staged")
+            nc.scalar.copy(staged[:], bank[:])
+            nc.sync.dma_start(out_view[:, :, group_start[g] * P : group_start[g] * P + width], staged[:])
+
+        for c in chunks:
+            ea, db, rest = [work[c][:, k] for k in range(3)]
+            if c >= 4:
+                rest = chunk_tile(c)[:, 2]
+                for t in range(PACK):
+                    fetch(rest, t, y[t], sc_list, c)
+            clash = keep.tile([P, PACK, widths[c]], F32, name="clash", tag="w1_codes", align_bytes=64)[:]
+            nc.vector.tensor_tensor(clash, ea, db, ALU.min)
+            nc.vector.tensor_scalar(clash, clash, -1.3, None, ALU.mult)
+            parts = [db, ea, rest, clash]
+            if c < 4:
+                parts = [db, ea, rest]
+                for t in range(PACK):
+                    nc.vector.tensor_tensor(rest[:, t, :], y[t][:].indirect(chunk_offsets(sc_list, c)), clash[:, t, :], ALU.add)
+            if c + 1 < len(CHUNK_BLOCKS):
+                work.append(chunk_tile(c + 1))
+                for t in range(PACK):
+                    fetch(work[c + 1][:, 1], t, yd[t], rb_list, c + 1)
+                for t in range(PACK):
+                    fetch(work[c + 1][:, 0], t, ye[t], ra_list, c + 1)
+            for b in range(CHUNK_BLOCKS[c]):
+                cols = slice(b * P, (b + 1) * P)
+                block = starts[c] // P + b
+                finish_block(block, [part[:, :, cols] for part in parts])
+                g = group_of[block]
+                if block + 1 == group_start[g] + GROUP_BLOCKS[g]:
+                    finish_group(g)

@@ -19,8 +19,13 @@ ACT = mybir.ActivationFunctionType
 P = 128
 PACK = 4
 STRIPE = 16
-CHUNK_BLOCKS = (2, 2, 2, 2)
+QUADRANT = 32
+LINE = 4
+CLASH_WEIGHT = -1.3
+CHUNK_BLOCKS = (3, 2, 2, 1)
 GROUP_BLOCKS = (2, 2, 2, 1, 1)
+EARLY_CHUNK = 2
+W3_SCALAR_COLUMNS = 48
 
 
 def tile_picked_yscafld_gelu_p_kernel(
@@ -30,7 +35,7 @@ def tile_picked_yscafld_gelu_p_kernel(
     with ExitStack() as ctx:
         keep = ctx.enter_context(tc.tile_pool(name="keep", bufs=1))
         ring = ctx.enter_context(tc.tile_pool(name="ring", bufs=3))
-        prod_psum = ctx.enter_context(tc.psum_pool(name="prod_psum", bufs=2))
+        result_psum = ctx.enter_context(tc.psum_pool(name="result_psum", bufs=2))
         sum_psum = ctx.enter_context(tc.psum_pool(name="sum_psum", bufs=4))
         back_psum = ctx.enter_context(tc.psum_pool(name="back_psum", bufs=2))
 
@@ -50,15 +55,16 @@ def tile_picked_yscafld_gelu_p_kernel(
             return tile
 
         def load_scales(tile, src):
-            for row in range(4):
-                nc.sync.dma_start(tile[row:P:32, :].bitcast(I32), src[0, row:16:4, :].bitcast(I32))
+            for row in range(PACK):
+                nc.sync.dma_start(tile[row:P:QUADRANT, :].bitcast(I32), src[0, row : 4 * PACK : PACK, :].bitcast(I32))
 
-        def load_scales_everywhere(name, src):
+        def load_scales_repeated(name, src):
             tile = keep.tile([P, src.shape[2]], U8, name=name + "_scales", align_bytes=64)
-            for quad in range(4):
-                rows = src[0, 4 * quad : 4 * quad + 4, :].bitcast(I32)
+            for quad in range(P // QUADRANT):
+                rows = src[0, PACK * quad : PACK * (quad + 1), :].bitcast(I32)
                 nc.sync.dma_start(
-                    tile[32 * quad : 32 * quad + 32, :].bitcast(I32), rows.unsqueeze(0).to_broadcast([8] + list(rows.shape))
+                    tile[QUADRANT * quad : QUADRANT * (quad + 1), :].bitcast(I32),
+                    rows.unsqueeze(0).to_broadcast([QUADRANT // PACK] + list(rows.shape)),
                 )
             return tile
 
@@ -68,7 +74,7 @@ def tile_picked_yscafld_gelu_p_kernel(
             return tile
 
         def pick_columns(name, words, scales, offsets):
-            codes = keep.tile([P, S], U32, name=name + "_codes", align_bytes=64)
+            codes = keep.tile([P, S], U32, name=name + "_codes", tag=name + "_codes", align_bytes=64)
             nc.vector.tensor_copy(codes[:], words[:].bitcast(U32).indirect(offsets[:]))
             plane = keep.tile([P, S], U8, name=name + "_plane", align_bytes=64)
             nc.vector.tensor_copy(plane[:], scales[:].indirect(offsets[:]))
@@ -77,53 +83,68 @@ def tile_picked_yscafld_gelu_p_kernel(
         def quantize(name, rounded):
             width = rounded.shape[1] // PACK
             codes = keep.tile([P, width], U32, name=name + "_codes", tag=name + "_codes", align_bytes=64)
-            plane = keep.tile([P, width], U8, name=name + "_plane", align_bytes=64)
+            plane = keep.tile([P, width], U8, name=name + "_plane", tag=name + "_plane", align_bytes=64)
             nc.vector.quantize_mx(out=codes[:].bitcast(FP8X4), scales=plane[:], in_=rounded)
             return codes, plane
 
-        def dealt_views(name, raw):
+        def quantize_dealt(name, raw, scalar_columns):
             rounded = keep.tile([P, H * PACK], BF16, name=name + "_bf16", align_bytes=64)
             dst = rounded[:].rearrange("p (t m j) -> p m j t", t=PACK, j=PACK)
             src = raw[:].rearrange("p j (m t) -> p m j t", t=PACK)
-            return rounded, dst, src
+            if scalar_columns:
+                nc.scalar.copy(dst[:, :scalar_columns], src[:, :scalar_columns])
+            nc.vector.tensor_copy(dst[:, scalar_columns:], src[:, scalar_columns:])
+            return quantize(name, rounded[:])
 
-        def product_tile(name, t, weight, picked, engine, pool):
-            cols = slice(t * P, (t + 1) * P)
-            bank = pool.tile([P, S], F32, name="bank")
+        def multiply(bank, stationary, cols, moving):
             nc.tensor.matmul_mx(
-                out=bank[:],
-                lhsT=weight[0][:, cols].bitcast(FP8X4),
-                lhsT_scale=weight[1][:, cols],
-                rhs=picked[0][:].bitcast(FP8X4),
-                rhs_scale=picked[1][:],
+                out=bank,
+                lhsT=stationary[0][:, cols].bitcast(FP8X4),
+                lhsT_scale=stationary[1][:, cols],
+                rhs=moving[0][:].bitcast(FP8X4),
+                rhs_scale=moving[1][:],
                 start=True,
                 stop=True,
             )
-            window = keep.tile([P, S], F32, name="%s_%d" % (name, t), align_bytes=64)
-            if engine is nc.scalar:
-                nc.scalar.copy(window[:], bank[:])
-            else:
-                nc.vector.tensor_copy(window[:], bank[:])
-            return window
+
+        def product_slabs(name, weight, picked, pools, empty_bank):
+            windows = []
+            for t in range(PACK):
+                bank = pools[t].tile([P, S], F32, name="bank")
+                multiply(bank[:], weight, slice(t * P, (t + 1) * P), picked)
+                window = keep.tile([P, S], F32, name="%s_%d" % (name, t), align_bytes=64)
+                empty_bank(window[:], bank[:])
+                windows.append(window)
+            return windows
 
         starts = [P * sum(CHUNK_BLOCKS[:c]) for c in range(len(CHUNK_BLOCKS))]
         widths = [P * blocks for blocks in CHUNK_BLOCKS]
+        last_chunk = len(CHUNK_BLOCKS) - 1
 
-        def chunk_offsets(offsets, c):
-            return offsets[:, starts[c] // STRIPE : (starts[c] + widths[c]) // STRIPE]
+        def looked_up(window, offsets, c):
+            return window[:].indirect(offsets[:, starts[c] // STRIPE : (starts[c] + widths[c]) // STRIPE])
 
-        def chunk_tile(c):
-            return ring.tile([P, 3, PACK, widths[c]], F32, name="work", bufs=2, align_bytes=64)
+        def work_tile(c):
+            tag = ("work", "e_picked_codes")[c % 2]
+            return keep.tile([P, 3, PACK, widths[c]], F32, name="work", tag=tag, align_bytes=64)
 
-        def fetch(dst, t, window, offsets, c):
-            nc.scalar.activation(dst[:, t, :], window[:].indirect(chunk_offsets(offsets, c)), ACT.Copy)
+        def clash_tile(c):
+            tag = ("w1_codes", "w1_plane")[c % 2]
+            return keep.tile([P, PACK, widths[c]], F32, name="clash", tag=tag, align_bytes=64)[:]
+
+        def fetch(dst, windows, offsets, c):
+            for t in range(PACK):
+                nc.scalar.activation(dst[:, t, :], looked_up(windows[t], offsets, c), ACT.Copy)
+
+        def flat(slabs):
+            return slabs.rearrange("p t r -> p (t r)")
 
         e_scale_tile = clear_scales("e", e_scales)
         x_scale_tile = clear_scales("x", x_scales)
 
         d_word_tile = load_words("d", d_words)
         grb_list = load_list("grb_list", grb)
-        d_scale_tile = load_scales_everywhere("d", d_scales)
+        d_scale_tile = load_scales_repeated("d", d_scales)
         w3_raw = load_weight("w3", w3)
         e_word_tile = load_words("e", e_words)
         gra_list = load_list("gra_list", gra)
@@ -143,113 +164,122 @@ def tile_picked_yscafld_gelu_p_kernel(
         identity = keep.tile([P, P], F32, name="identity")
         make_identity(nc, identity[:])
 
-        chunks = range(len(CHUNK_BLOCKS))
-        work = [chunk_tile(0)]
-        ea = [work[0][:, 0]]
-        db = [work[0][:, 1]]
+        work = [work_tile(0)]
+        db_of = [work[0][:, 1]]
 
         d_picked = pick_columns("d_picked", d_word_tile, d_scale_tile, grb_list)
-        rounded, dst, src = dealt_views("w3", w3_raw)
-        nc.scalar.copy(dst[:, :48], src[:, :48])
-        nc.vector.tensor_copy(dst[:, 48:], src[:, 48:])
-        w3_q = quantize("w3", rounded[:])
-        yd = [product_tile("yd", t, w3_q, d_picked, engine, (sum_psum, sum_psum, sum_psum, sum_psum)[t]) for t, engine in enumerate((nc.scalar, nc.scalar, nc.scalar, nc.scalar))]
-        for t in range(PACK):
-            fetch(db[0], t, yd[t], rb_list, 0)
+        w3_q = quantize_dealt("w3", w3_raw, W3_SCALAR_COLUMNS)
+        yd = product_slabs("yd", w3_q, d_picked, [sum_psum] * PACK, nc.scalar.copy)
+        fetch(db_of[0], yd, rb_list, 0)
 
         e_picked = pick_columns("e_picked", e_word_tile, e_scale_tile, gra_list)
-        rounded, dst, src = dealt_views("w2", w2_raw)
-        nc.vector.tensor_copy(dst, src)
-        w2_q = quantize("w2", rounded[:])
-        ye = [product_tile("ye", t, w2_q, e_picked, engine, (prod_psum, prod_psum, back_psum, back_psum)[t]) for t, engine in enumerate((nc.scalar, nc.scalar, nc.scalar, nc.scalar))]
-        for t in range(PACK):
-            fetch(ea[0], t, ye[t], ra_list, 0)
+        w2_q = quantize_dealt("w2", w2_raw, 0)
+        ye = product_slabs("ye", w2_q, e_picked, [result_psum, result_psum, back_psum, back_psum], nc.scalar.copy)
+        fetch(work[0][:, 0], ye, ra_list, 0)
 
         x_picked = pick_columns("x_picked", x_word_tile, x_scale_tile, offs_list)
-        rounded, dst, src = dealt_views("w1", w1_raw)
-        nc.vector.tensor_copy(dst, src)
-        w1_q = quantize("w1", rounded[:])
-        y = [product_tile("y", t, w1_q, x_picked, engine, (sum_psum, sum_psum, sum_psum, sum_psum)[t]) for t, engine in enumerate((nc.vector, nc.vector, nc.vector, nc.vector))]
+        w1_q = quantize_dealt("w1", w1_raw, 0)
+        y = product_slabs("y", w1_q, x_picked, [sum_psum] * PACK, nc.vector.tensor_copy)
 
-        rounded = keep.tile([P, N * PACK], BF16, name="w4_bf16", align_bytes=64)
-        dst = rounded[:].rearrange("p (c i j) -> p c j i", i=4, j=PACK)
-        src = w4_raw[:].rearrange("p j (c i) -> p c j i", i=4)
-        nc.vector.tensor_copy(dst, src)
-        w4_q = quantize("w4", rounded[:])
+        w4_rounded = keep.tile([P, N * PACK], BF16, name="w4_bf16", align_bytes=64)
+        nc.vector.tensor_copy(
+            w4_rounded[:].rearrange("p (c i j) -> p c j i", i=LINE, j=PACK),
+            w4_raw[:].rearrange("p j (c i) -> p c j i", i=LINE),
+        )
+        w4_q = quantize("w4", w4_rounded[:])
 
         group_of = [g for g, blocks in enumerate(GROUP_BLOCKS) for b in range(blocks)]
         group_start = [sum(GROUP_BLOCKS[:g]) for g in range(len(GROUP_BLOCKS))]
         hid = [
             keep.tile([P, blocks * P * PACK], BF16, name="hid%d" % g, align_bytes=64) for g, blocks in enumerate(GROUP_BLOCKS)
         ]
-        unit_spread = unit_tile[:].unsqueeze(1).to_broadcast([P, P, PACK])
         out_view = out.rearrange("(h p) r -> p h r", p=P)
+        full_groups = []
 
-        def finish_block(block, parts):
+        def hid_block(block):
+            g = group_of[block]
+            place = block - group_start[g]
+            if place + 1 == GROUP_BLOCKS[g]:
+                full_groups.append(g)
+            return hid[g][:, place * P * PACK : (place + 1) * P * PACK]
+
+        def finish_groups():
+            for g in full_groups:
+                width = GROUP_BLOCKS[g] * P
+                hid_q = quantize("hid%d" % g, hid[g][:])
+                bank = result_psum.tile([P, N // P, width], F32, name="result", tag="bank")
+                for h in range(N // P):
+                    multiply(bank[:, h, :], w4_q, slice(h * P, (h + 1) * P), hid_q)
+                staged = ring.tile([P, N // P, width], F32, name="staged")
+                nc.scalar.copy(staged[:], bank[:])
+                nc.sync.dma_start(out_view[:, :, group_start[g] * P : group_start[g] * P + width], staged[:])
+            full_groups.clear()
+
+        def sum_by_transposes(block, terms, cols):
             total = sum_psum.tile([P, PACK, P], F32, name="total", tag="bank")
-            for k, part in enumerate(parts):
-                for t in range(PACK):
-                    nc.tensor.matmul(
-                        total[:, t, :],
-                        part[:, t, :],
-                        identity[:],
-                        start=(k == 0 and t == 0),
-                        stop=(k == len(parts) - 1 and t == PACK - 1),
-                        is_transpose=True,
-                    )
+            passes = [(term, t) for term in terms for t in range(PACK)]
+            for k, (term, t) in enumerate(passes):
+                nc.tensor.matmul(
+                    total[:, t, :],
+                    term[:, t, cols],
+                    identity[:],
+                    start=(k == 0),
+                    stop=(k == len(passes) - 1),
+                    is_transpose=True,
+                )
             smooth = ring.tile([P, PACK, P], F32, name="smooth", align_bytes=64)
             nc.scalar.activation(smooth[:], total[:], ACT.Gelu_apprx_tanh)
             back = back_psum.tile([P, PACK, P], F32, name="back", tag="bank")
             for t in range(PACK):
                 nc.tensor.transpose(back[:, t, :], smooth[:, t, :], identity[:])
-            g = group_of[block]
-            place = block - group_start[g]
-            dst = hid[g][:, place * P * PACK : (place + 1) * P * PACK].rearrange("p (r t) -> p r t", t=PACK)
-            nc.vector.tensor_tensor(dst, back[:].rearrange("p t r -> p r t"), unit_spread, ALU.mult)
+            nc.vector.tensor_tensor(
+                hid_block(block).rearrange("p (r t) -> p r t", t=PACK),
+                back[:].rearrange("p t r -> p r t"),
+                unit_tile[:].unsqueeze(1).to_broadcast([P, P, PACK]),
+                ALU.mult,
+            )
 
-        def finish_group(g):
-            width = GROUP_BLOCKS[g] * P
-            codes, plane = quantize("hid%d" % g, hid[g][:])
-            bank = prod_psum.tile([P, N // P, width], F32, name="result", tag="bank")
-            for h in range(N // P):
-                cols = slice(h * P, (h + 1) * P)
-                nc.tensor.matmul_mx(
-                    out=bank[:, h, :],
-                    lhsT=w4_q[0][:, cols].bitcast(FP8X4),
-                    lhsT_scale=w4_q[1][:, cols],
-                    rhs=codes[:].bitcast(FP8X4),
-                    rhs_scale=plane[:],
-                    start=True,
-                    stop=True,
-                )
-            staged = ring.tile([P, N // P, width], F32, name="staged")
-            nc.scalar.copy(staged[:], bank[:])
-            nc.sync.dma_start(out_view[:, :, group_start[g] * P : group_start[g] * P + width], staged[:])
-
-        for c in chunks:
-            ea, db, rest = [work[c][:, k] for k in range(3)]
-            if c >= 4:
-                rest = chunk_tile(c)[:, 2]
-                for t in range(PACK):
-                    fetch(rest, t, y[t], sc_list, c)
-            clash = keep.tile([P, PACK, widths[c]], F32, name="clash", tag="w1_codes", align_bytes=64)[:]
+        for c in range(last_chunk):
+            ea, db, with_ea = work[c][:, 0], db_of[c], work[c][:, 2]
+            clash = clash_tile(c)
+            fold_db = c == last_chunk - 1
             nc.vector.tensor_tensor(clash, ea, db, ALU.min)
-            nc.vector.tensor_scalar(clash, clash, -1.3, None, ALU.mult)
-            parts = [db, ea, rest, clash]
-            if c < 4:
-                parts = [db, ea, rest]
-                for t in range(PACK):
-                    nc.vector.tensor_tensor(rest[:, t, :], y[t][:].indirect(chunk_offsets(sc_list, c)), clash[:, t, :], ALU.add)
-            if c + 1 < len(CHUNK_BLOCKS):
-                work.append(chunk_tile(c + 1))
-                for t in range(PACK):
-                    fetch(work[c + 1][:, 1], t, yd[t], rb_list, c + 1)
-                for t in range(PACK):
-                    fetch(work[c + 1][:, 0], t, ye[t], ra_list, c + 1)
+            for t in range(PACK):
+                nc.vector.tensor_tensor(with_ea[:, t, :], looked_up(y[t], sc_list, c), ea[:, t, :], ALU.add)
+                if t == 0 and fold_db:
+                    nc.vector.scalar_tensor_tensor(flat(clash), flat(clash), CLASH_WEIGHT, flat(db), ALU.mult, ALU.add)
+                elif t == 0:
+                    nc.vector.tensor_scalar(clash, clash, CLASH_WEIGHT, None, ALU.mult)
+            finish_groups()
+
+            work.append(work_tile(c + 1))
+            if c + 1 == EARLY_CHUNK:
+                early = keep.tile([P, PACK, widths[c + 1]], F32, name="early", tag="x_picked_codes", align_bytes=64)
+                db_of.append(early[:])
+            else:
+                db_of.append(work[c + 1][:, 1])
+            fetch(db_of[c + 1], yd, rb_list, c + 1)
+            fetch(work[c + 1][:, 0], ye, ra_list, c + 1)
+
             for b in range(CHUNK_BLOCKS[c]):
-                cols = slice(b * P, (b + 1) * P)
-                block = starts[c] // P + b
-                finish_block(block, [part[:, :, cols] for part in parts])
-                g = group_of[block]
-                if block + 1 == group_start[g] + GROUP_BLOCKS[g]:
-                    finish_group(g)
+                terms = [clash, with_ea] if fold_db else [db, clash, with_ea]
+                sum_by_transposes(starts[c] // P + b, terms, slice(b * P, (b + 1) * P))
+
+        ea, db, mol = work[last_chunk][:, 0], db_of[last_chunk], work[last_chunk][:, 2]
+        clash = clash_tile(last_chunk)
+        sides = keep.tile([P, PACK, P], F32, name="sides", align_bytes=64)[:]
+        nc.vector.tensor_tensor(clash, ea, db, ALU.min)
+        nc.vector.tensor_tensor(sides, ea, db, ALU.add)
+        nc.vector.scalar_tensor_tensor(flat(clash), flat(clash), CLASH_WEIGHT, flat(sides), ALU.mult, ALU.add)
+        smooth_last = keep.tile([P, PACK, P], F32, name="smooth_last", align_bytes=64)
+        for t in range(PACK):
+            nc.vector.tensor_tensor(mol[:, t, :], looked_up(y[t], sc_list, last_chunk), clash[:, t, :], ALU.add)
+            nc.scalar.activation(smooth_last[:, t, :], mol[:, t, :], ACT.Gelu_apprx_tanh)
+        finish_groups()
+        nc.vector.tensor_tensor(
+            hid_block(starts[last_chunk] // P).rearrange("p (c i t) -> p c t i", i=LINE, t=PACK),
+            smooth_last[:].rearrange("p t (c i) -> p c t i", i=LINE),
+            unit_tile[:].unsqueeze(1).unsqueeze(3).to_broadcast([P, P // LINE, PACK, LINE]),
+            ALU.mult,
+        )
+        finish_groups()

from contextlib import ExitStack

import concourse.mybir as mybir
from concourse.masks import make_identity

K, S, N, H, U = 512, 512, 256, 512, 1024
FLOPS = 2 * (3 * K * H * S + H * N * U)

F32 = mybir.dt.float32
BF16 = mybir.dt.bfloat16
I32 = mybir.dt.int32
U32 = mybir.dt.uint32
U16 = mybir.dt.uint16
U8 = mybir.dt.uint8
FP8X4 = mybir.dt.float8_e4m3fn_x4
ALU = mybir.AluOpType
ACT = mybir.ActivationFunctionType

P = 128
PACK = 4
STRIPE = 16
QUADRANT = 32
LINE = 4
CLASH_WEIGHT = -1.3
CHUNK_BLOCKS = (3, 2, 2, 1)
GROUP_BLOCKS = (2, 2, 2, 1, 1)
EARLY_CHUNK = 2
W3_SCALAR_COLUMNS = 48


def tile_picked_yscafld_gelu_p_kernel(
    tc, x_words, x_scales, w1, e_words, e_scales, w2, d_words, d_scales, w3, unit, w4, offs, gra, grb, sc_, ra, rb, out
):
    nc = tc.nc
    with ExitStack() as ctx:
        keep = ctx.enter_context(tc.tile_pool(name="keep", bufs=1))
        ring = ctx.enter_context(tc.tile_pool(name="ring", bufs=3))
        result_psum = ctx.enter_context(tc.psum_pool(name="result_psum", bufs=2))
        sum_psum = ctx.enter_context(tc.psum_pool(name="sum_psum", bufs=4))
        back_psum = ctx.enter_context(tc.psum_pool(name="back_psum", bufs=2))

        def load_list(name, src):
            tile = keep.tile(list(src.shape), U16, name=name)
            nc.sync.dma_start(tile[:], src)
            return tile

        def load_words(name, src):
            tile = keep.tile([P, src.shape[2]], I32, name=name + "_words", align_bytes=64)
            nc.sync.dma_start(tile[:], src[0].rearrange("p c r -> p (c r)").bitcast(I32))
            return tile

        def clear_scales(name, src):
            tile = keep.tile([P, src.shape[2]], U8, name=name + "_scales", align_bytes=64)
            nc.vector.memset(tile[:].bitcast(I32), 0)
            return tile

        def load_scales(tile, src):
            for row in range(PACK):
                nc.sync.dma_start(tile[row:P:QUADRANT, :].bitcast(I32), src[0, row : 4 * PACK : PACK, :].bitcast(I32))

        def load_scales_repeated(name, src):
            tile = keep.tile([P, src.shape[2]], U8, name=name + "_scales", align_bytes=64)
            for quad in range(P // QUADRANT):
                rows = src[0, PACK * quad : PACK * (quad + 1), :].bitcast(I32)
                nc.sync.dma_start(
                    tile[QUADRANT * quad : QUADRANT * (quad + 1), :].bitcast(I32),
                    rows.unsqueeze(0).to_broadcast([QUADRANT // PACK] + list(rows.shape)),
                )
            return tile

        def load_weight(name, src):
            tile = keep.tile([P, PACK, src.shape[1]], F32, name=name + "_raw", align_bytes=64)
            nc.sync.dma_start(tile[:], src.rearrange("(p j) c -> p j c", j=PACK))
            return tile

        def pick_columns(name, words, scales, offsets):
            codes = keep.tile([P, S], U32, name=name + "_codes", tag=name + "_codes", align_bytes=64)
            nc.vector.tensor_copy(codes[:], words[:].bitcast(U32).indirect(offsets[:]))
            plane = keep.tile([P, S], U8, name=name + "_plane", align_bytes=64)
            nc.vector.tensor_copy(plane[:], scales[:].indirect(offsets[:]))
            return codes, plane

        def quantize(name, rounded):
            width = rounded.shape[1] // PACK
            codes = keep.tile([P, width], U32, name=name + "_codes", tag=name + "_codes", align_bytes=64)
            plane = keep.tile([P, width], U8, name=name + "_plane", tag=name + "_plane", align_bytes=64)
            nc.vector.quantize_mx(out=codes[:].bitcast(FP8X4), scales=plane[:], in_=rounded)
            return codes, plane

        def quantize_dealt(name, raw, scalar_columns):
            rounded = keep.tile([P, H * PACK], BF16, name=name + "_bf16", align_bytes=64)
            dst = rounded[:].rearrange("p (t m j) -> p m j t", t=PACK, j=PACK)
            src = raw[:].rearrange("p j (m t) -> p m j t", t=PACK)
            if scalar_columns:
                nc.scalar.copy(dst[:, :scalar_columns], src[:, :scalar_columns])
            nc.vector.tensor_copy(dst[:, scalar_columns:], src[:, scalar_columns:])
            return quantize(name, rounded[:])

        def multiply(bank, stationary, cols, moving):
            nc.tensor.matmul_mx(
                out=bank,
                lhsT=stationary[0][:, cols].bitcast(FP8X4),
                lhsT_scale=stationary[1][:, cols],
                rhs=moving[0][:].bitcast(FP8X4),
                rhs_scale=moving[1][:],
                start=True,
                stop=True,
            )

        def product_slabs(name, weight, picked, pools, empty_bank):
            windows = []
            for t in range(PACK):
                bank = pools[t].tile([P, S], F32, name="bank")
                multiply(bank[:], weight, slice(t * P, (t + 1) * P), picked)
                window = keep.tile([P, S], F32, name="%s_%d" % (name, t), align_bytes=64)
                empty_bank(window[:], bank[:])
                windows.append(window)
            return windows

        starts = [P * sum(CHUNK_BLOCKS[:c]) for c in range(len(CHUNK_BLOCKS))]
        widths = [P * blocks for blocks in CHUNK_BLOCKS]
        last_chunk = len(CHUNK_BLOCKS) - 1

        def looked_up(window, offsets, c):
            return window[:].indirect(offsets[:, starts[c] // STRIPE : (starts[c] + widths[c]) // STRIPE])

        def work_tile(c):
            tag = ("work", "e_picked_codes")[c % 2]
            return keep.tile([P, 3, PACK, widths[c]], F32, name="work", tag=tag, align_bytes=64)

        def clash_tile(c):
            tag = ("w1_codes", "w1_plane")[c % 2]
            return keep.tile([P, PACK, widths[c]], F32, name="clash", tag=tag, align_bytes=64)[:]

        def fetch(dst, windows, offsets, c):
            for t in range(PACK):
                nc.scalar.activation(dst[:, t, :], looked_up(windows[t], offsets, c), ACT.Copy)

        def flat(slabs):
            return slabs.rearrange("p t r -> p (t r)")

        e_scale_tile = clear_scales("e", e_scales)
        x_scale_tile = clear_scales("x", x_scales)

        d_word_tile = load_words("d", d_words)
        grb_list = load_list("grb_list", grb)
        d_scale_tile = load_scales_repeated("d", d_scales)
        w3_raw = load_weight("w3", w3)
        e_word_tile = load_words("e", e_words)
        gra_list = load_list("gra_list", gra)
        rb_list = load_list("rb_list", rb)
        load_scales(e_scale_tile, e_scales)
        w2_raw = load_weight("w2", w2)
        x_word_tile = load_words("x", x_words)
        offs_list = load_list("offs_list", offs)
        ra_list = load_list("ra_list", ra)
        load_scales(x_scale_tile, x_scales)
        w1_raw = load_weight("w1", w1)
        sc_list = load_list("sc_list", sc_)
        w4_raw = load_weight("w4", w4)
        unit_tile = keep.tile([P, PACK], F32, name="unit_tile")
        nc.sync.dma_start(unit_tile[:], unit.rearrange("(p t) o -> p (t o)", t=PACK))

        identity = keep.tile([P, P], F32, name="identity")
        make_identity(nc, identity[:])

        work = [work_tile(0)]
        db_of = [work[0][:, 1]]

        d_picked = pick_columns("d_picked", d_word_tile, d_scale_tile, grb_list)
        w3_q = quantize_dealt("w3", w3_raw, W3_SCALAR_COLUMNS)
        yd = product_slabs("yd", w3_q, d_picked, [sum_psum] * PACK, nc.scalar.copy)
        fetch(db_of[0], yd, rb_list, 0)

        e_picked = pick_columns("e_picked", e_word_tile, e_scale_tile, gra_list)
        w2_q = quantize_dealt("w2", w2_raw, 0)
        ye = product_slabs("ye", w2_q, e_picked, [result_psum, result_psum, back_psum, back_psum], nc.scalar.copy)
        fetch(work[0][:, 0], ye, ra_list, 0)

        x_picked = pick_columns("x_picked", x_word_tile, x_scale_tile, offs_list)
        w1_q = quantize_dealt("w1", w1_raw, 0)
        y = product_slabs("y", w1_q, x_picked, [sum_psum] * PACK, nc.vector.tensor_copy)

        w4_rounded = keep.tile([P, N * PACK], BF16, name="w4_bf16", align_bytes=64)
        nc.vector.tensor_copy(
            w4_rounded[:].rearrange("p (c i j) -> p c j i", i=LINE, j=PACK),
            w4_raw[:].rearrange("p j (c i) -> p c j i", i=LINE),
        )
        w4_q = quantize("w4", w4_rounded[:])

        group_of = [g for g, blocks in enumerate(GROUP_BLOCKS) for b in range(blocks)]
        group_start = [sum(GROUP_BLOCKS[:g]) for g in range(len(GROUP_BLOCKS))]
        hid = [
            keep.tile([P, blocks * P * PACK], BF16, name="hid%d" % g, align_bytes=64) for g, blocks in enumerate(GROUP_BLOCKS)
        ]
        out_view = out.rearrange("(h p) r -> p h r", p=P)
        full_groups = []

        def hid_block(block):
            g = group_of[block]
            place = block - group_start[g]
            if place + 1 == GROUP_BLOCKS[g]:
                full_groups.append(g)
            return hid[g][:, place * P * PACK : (place + 1) * P * PACK]

        def finish_groups():
            for g in full_groups:
                width = GROUP_BLOCKS[g] * P
                hid_q = quantize("hid%d" % g, hid[g][:])
                bank = result_psum.tile([P, N // P, width], F32, name="result", tag="bank")
                for h in range(N // P):
                    multiply(bank[:, h, :], w4_q, slice(h * P, (h + 1) * P), hid_q)
                staged = ring.tile([P, N // P, width], F32, name="staged")
                nc.scalar.copy(staged[:], bank[:])
                nc.sync.dma_start(out_view[:, :, group_start[g] * P : group_start[g] * P + width], staged[:])
            full_groups.clear()

        def sum_by_transposes(block, terms, cols):
            total = sum_psum.tile([P, PACK, P], F32, name="total", tag="bank")
            passes = [(term, t) for term in terms for t in range(PACK)]
            for k, (term, t) in enumerate(passes):
                nc.tensor.matmul(
                    total[:, t, :],
                    term[:, t, cols],
                    identity[:],
                    start=(k == 0),
                    stop=(k == len(passes) - 1),
                    is_transpose=True,
                )
            smooth = ring.tile([P, PACK, P], F32, name="smooth", align_bytes=64)
            nc.scalar.activation(smooth[:], total[:], ACT.Gelu_apprx_tanh)
            back = back_psum.tile([P, PACK, P], F32, name="back", tag="bank")
            for t in range(PACK):
                nc.tensor.transpose(back[:, t, :], smooth[:, t, :], identity[:])
            nc.vector.tensor_tensor(
                hid_block(block).rearrange("p (r t) -> p r t", t=PACK),
                back[:].rearrange("p t r -> p r t"),
                unit_tile[:].unsqueeze(1).to_broadcast([P, P, PACK]),
                ALU.mult,
            )

        for c in range(last_chunk):
            ea, db, with_ea = work[c][:, 0], db_of[c], work[c][:, 2]
            clash = clash_tile(c)
            fold_db = c == last_chunk - 1
            nc.vector.tensor_tensor(clash, ea, db, ALU.min)
            for t in range(PACK):
                nc.vector.tensor_tensor(with_ea[:, t, :], looked_up(y[t], sc_list, c), ea[:, t, :], ALU.add)
                if t == 0 and fold_db:
                    nc.vector.scalar_tensor_tensor(flat(clash), flat(clash), CLASH_WEIGHT, flat(db), ALU.mult, ALU.add)
                elif t == 0:
                    nc.vector.tensor_scalar(clash, clash, CLASH_WEIGHT, None, ALU.mult)
            finish_groups()

            work.append(work_tile(c + 1))
            if c + 1 == EARLY_CHUNK:
                early = keep.tile([P, PACK, widths[c + 1]], F32, name="early", tag="x_picked_codes", align_bytes=64)
                db_of.append(early[:])
            else:
                db_of.append(work[c + 1][:, 1])
            fetch(db_of[c + 1], yd, rb_list, c + 1)
            fetch(work[c + 1][:, 0], ye, ra_list, c + 1)

            for b in range(CHUNK_BLOCKS[c]):
                terms = [clash, with_ea] if fold_db else [db, clash, with_ea]
                sum_by_transposes(starts[c] // P + b, terms, slice(b * P, (b + 1) * P))

        ea, db, mol = work[last_chunk][:, 0], db_of[last_chunk], work[last_chunk][:, 2]
        clash = clash_tile(last_chunk)
        sides = keep.tile([P, PACK, P], F32, name="sides", align_bytes=64)[:]
        nc.vector.tensor_tensor(clash, ea, db, ALU.min)
        nc.vector.tensor_tensor(sides, ea, db, ALU.add)
        nc.vector.scalar_tensor_tensor(flat(clash), flat(clash), CLASH_WEIGHT, flat(sides), ALU.mult, ALU.add)
        smooth_last = keep.tile([P, PACK, P], F32, name="smooth_last", align_bytes=64)
        for t in range(PACK):
            nc.vector.tensor_tensor(mol[:, t, :], looked_up(y[t], sc_list, last_chunk), clash[:, t, :], ALU.add)
            nc.scalar.activation(smooth_last[:, t, :], mol[:, t, :], ACT.Gelu_apprx_tanh)
        finish_groups()
        nc.vector.tensor_tensor(
            hid_block(starts[last_chunk] // P).rearrange("p (c i t) -> p c t i", i=LINE, t=PACK),
            smooth_last[:].rearrange("p t (c i) -> p c t i", i=LINE),
            unit_tile[:].unsqueeze(1).unsqueeze(3).to_broadcast([P, P // LINE, PACK, LINE]),
            ALU.mult,
        )
        finish_groups()
